import numpy as np
import ml_dtypes


def mxq(x, axis, fmt="e4m3"):
    dtype, down = {"e4m3": (ml_dtypes.float8_e4m3fn, 7), "e5m2": (ml_dtypes.float8_e5m2, 14)}[fmt]
    v = np.moveaxis(np.asarray(x, np.float32).astype(ml_dtypes.bfloat16).astype(np.float64), axis, -1)
    blocks = v.reshape(v.shape[:-1] + (-1, 32))
    amax = np.abs(blocks).max(-1, keepdims=True)
    byte = np.maximum(np.where(amax > 0, np.frexp(amax)[1] - 1 + 127, 0) - down, 1)
    scale = np.exp2(byte - 127.0)
    codes = (blocks / scale).astype(np.float32).astype(dtype).astype(np.float64)
    return np.moveaxis((codes * scale).reshape(v.shape), -1, axis)


WIDE = False


def mx_kscale(k):
    if not WIDE:
        return np.ones(k)
    levels = np.array([10, -10, 5, -5, 0])
    if k % 512:
        return np.exp2(np.random.permutation(np.resize(levels, k // 32))).repeat(32)
    a = np.empty((k // 512, 16))
    for p in range(k // 512):
        a[p, :8] = np.random.permutation(np.resize(levels, 8))
        for g in range(8):
            far = levels[np.abs(levels - a[p, g]) >= 10]
            a[p, g + 8] = far[np.random.randint(len(far))]
    return np.exp2(a.ravel()).repeat(32)


def f64(x):
    return np.asarray(x).astype(np.float64)


def striped(idx):
    return np.tile(idx.reshape(-1, 16).T, (8, 1)).astype(np.uint16)


def unstriped(offs):
    return offs[:16].T.reshape(-1).astype(np.int64)


def pack_weight(w):
    k, n = w.shape
    w = f64(np.asarray(w, np.float32).astype(ml_dtypes.bfloat16)).reshape(k // 32, 32, n)
    amax = np.abs(w).max(1)
    byte = np.clip(np.where(amax > 0, np.frexp(amax)[1] - 1 + 127 - 7, 1), 1, 254)
    scaled = (w * np.exp2(127.0 - byte)[:, None, :]).reshape(k, n).astype(np.float32)
    words = np.ascontiguousarray(scaled.reshape(k // 512, 128, 4, n).transpose(0, 1, 3, 2)).astype(ml_dtypes.float8_e4m3fn).view(np.uint8)
    return words, np.ascontiguousarray(byte.astype(np.uint8).reshape(k // 512, 16, n))


def unpack_weight(words, scales):
    g, p, n, _ = words.shape
    vals = np.ascontiguousarray(words).view(ml_dtypes.float8_e4m3fn).astype(np.float64) * np.repeat(np.exp2(scales.astype(np.float64) - 127.0), 8, axis=1)[..., None]
    return vals.transpose(0, 1, 3, 2).reshape(g * 512, n)


E2M1 = np.array([0.0, 0.5, 1.0, 1.5, 2.0, 3.0, 4.0, 6.0, -0.0, -0.5, -1.0, -1.5, -2.0, -3.0, -4.0, -6.0])


def pack_fp4(w):
    k, n = w.shape
    w = f64(np.asarray(w, np.float32).astype(ml_dtypes.bfloat16)).reshape(k // 32, 32, n)
    amax = np.abs(w).max(1)
    mant, ex = np.frexp(amax / 6.0)
    byte = np.clip(np.where(amax > 0, np.where(mant > 0.5, ex, ex - 1) + 127, 1), 1, 254)
    scaled = (w * np.exp2(127.0 - byte)[:, None, :]).reshape(k, n).astype(np.float32)
    c = np.ascontiguousarray(scaled.reshape(k // 512, 128, 4, n).transpose(0, 1, 3, 2)).astype(ml_dtypes.float4_e2m1fn).view(np.uint8) & 0xF
    words = (c[..., 0::2] | (c[..., 1::2] << 4)).reshape(k // 512, 128, 2 * n)
    return np.ascontiguousarray(words), np.ascontiguousarray(byte.astype(np.uint8).reshape(k // 512, 16, n))


def unpack_fp4(words, scales):
    g, _, n = scales.shape
    words = np.ascontiguousarray(words).reshape(g, 128, n, 2)
    nib = np.empty((g, 128, n, 4), np.uint8)
    nib[..., 0::2] = words & 0xF
    nib[..., 1::2] = words >> 4
    vals = E2M1[nib] * np.repeat(np.exp2(scales.astype(np.float64) - 127.0), 8, axis=1)[..., None]
    return vals.transpose(0, 1, 3, 2).reshape(g * 512, n)


def planes(y):
    n, m = y.shape
    v = y.astype(np.float32).astype(ml_dtypes.bfloat16).astype(np.float64).reshape(n // 32, 32, m)
    top = np.abs(v).max(1)
    byte = np.clip(np.where(top > 0, np.frexp(top)[1] - 1 + 127 - 7, 1), 1, 254)
    codes = (v * np.exp2(127.0 - byte)[:, None, :]).reshape(n, m).astype(np.float32).astype(ml_dtypes.float8_e4m3fn).view(np.uint8)
    words = codes.reshape(n // 512, 128, 4, m).transpose(0, 1, 3, 2)
    return np.ascontiguousarray(words), np.ascontiguousarray(byte.astype(np.uint8).reshape(n // 512, 16, m))


K, T, S, N, H, W = 512, 2048, 512, 512, 512, 2048


def setup_inputs():
    n = np.random.standard_normal
    s = mx_kscale(K)[:, None]
    u = mx_kscale(S)
    packed_xT = pack_weight(n((K, T)) * s)
    packed_w1 = pack_fp4(n((S, N)) / np.sqrt(S) / u[:, None])
    return {
        "x_words": packed_xT[0],
        "x_scales": packed_xT[1],
        "wa": (n((K, H)) / np.sqrt(K) / s).astype(np.float32),
        "gt": (np.random.uniform(0.5, 1.5, (S, 1)) * u[:, None]).astype(np.float32),
        "w1_words": packed_w1[0],
        "w1_scales": packed_w1[1],
        "tau": np.random.uniform(0.3, 0.9, (N, 1)).astype(np.float32),
        "offs": striped(np.random.permutation(T)[:S]),
        "n1": striped(np.random.permutation(H)),
        "n2": striped(np.random.permutation(H)),
        "n3": striped(np.random.permutation(H)),
        "n4": striped(np.random.randint(0, H, W)),
    }


def reference(x_words, x_scales, wa, gt, w1_words, w1_scales, tau, offs, n1, n2, n3, n4):
    xq = unpack_weight(x_words, x_scales)[:, unstriped(offs)]
    y = xq.T @ mxq(f64(wa), 0, "e4m3")
    z = f64(gt) * (0.75 * (y * y[:, unstriped(n1)] + y[:, unstriped(n2)] * y[:, unstriped(n3)]))
    h = unpack_fp4(w1_words, w1_scales).T @ mxq(z, 0, "e4m3")
    top = h.max(axis=1, keepdims=True)
    ea = np.exp(f64(tau) * (h[:, unstriped(n4)] - top))
    mx = ea.reshape(N, H, 4).max(axis=2)
    mn = ea.reshape(N, H, 4).min(axis=2)
    out_0 = 3.0 * (h * (mx - mn))
    return (out_0,) + planes(out_0)

@@ -1,0 +1,166 @@
+from contextlib import ExitStack
+
+import concourse.mybir as mybir
+
+K, T, S, N, H, W = 512, 2048, 512, 512, 512, 2048
+FLOPS = 2 * K * S * H + 2 * S * N * H
+
+F32 = mybir.dt.float32
+BF16 = mybir.dt.bfloat16
+I32 = mybir.dt.int32
+U32 = mybir.dt.uint32
+U16 = mybir.dt.uint16
+U8 = mybir.dt.uint8
+FP8X4 = mybir.dt.float8_e4m3fn_x4
+FP4X4 = mybir.dt.float4_e2m1fn_x4
+ALU = mybir.AluOpType
+ACT = mybir.ActivationFunctionType
+
+P = 128
+PACK = 4
+LIST_ROWS = 16
+CH = 128
+Z_CHUNKS = [(0, 256), (256, 128), (384, 128)]
+
+
+def tile_picked_tokdotegp_none_po_kernel(tc, x_words, x_scales, wa, gt, w1_words, w1_scales, tau, offs, n1, n2, n3, n4, out_0, out_1, out_2):
+    nc = tc.nc
+    with ExitStack() as ctx:
+        keep = ctx.enter_context(tc.tile_pool(name="keep", bufs=1))
+        ring = ctx.enter_context(tc.tile_pool(name="ring", bufs=3))
+        psum = ctx.enter_context(tc.psum_pool(name="psum", bufs=1))
+
+        offs_sb = keep.tile([P, S // LIST_ROWS], U16, name="offs_sb")
+        n1_sb = keep.tile([P, H // LIST_ROWS], U16, name="n1_sb")
+        n2_sb = keep.tile([P, H // LIST_ROWS], U16, name="n2_sb")
+        n3_sb = keep.tile([P, H // LIST_ROWS], U16, name="n3_sb")
+        n4_sb = keep.tile([P, W // LIST_ROWS], U16, name="n4_sb")
+        x_all = keep.tile([P, T], I32, name="x_all")
+        xs_all = keep.tile([P, T], U8, name="xs_all")
+        wa_raw = [keep.tile([P, PACK, H // 2], F32, name=f"wa_raw{u}") for u in range(2)]
+        w1_raw = keep.tile([P, 2 * N], U8, name="w1_raw")
+        w1s_raw = keep.tile([P, N], U8, name="w1s_raw")
+        gt_sb = keep.tile([P, PACK], F32, name="gt_sb")
+        tau_sb = keep.tile([P, PACK], F32, name="tau_sb")
+
+        nc.vector.memset(xs_all[:].bitcast(I32), 0)
+        nc.vector.memset(w1s_raw[:].bitcast(I32), 0)
+        nc.sync.dma_start(offs_sb[:], offs)
+        nc.sync.dma_start(x_all[:], x_words[0].rearrange("p c r -> p (c r)").bitcast(I32))
+        for q in range(4):
+            nc.scalar.dma_start(xs_all[32 * q : 32 * q + 4, :].bitcast(I32), x_scales[0, 4 * q : 4 * q + 4, :].bitcast(I32))
+        wa_rows = wa.rearrange("(p r) h -> p r h", r=PACK)
+        for u in range(2):
+            nc.sync.dma_start(wa_raw[u][:], wa_rows[:, :, u * (H // 2) : (u + 1) * (H // 2)])
+        nc.sync.dma_start(n3_sb[:], n3)
+        nc.sync.dma_start(n1_sb[:], n1)
+        nc.sync.dma_start(gt_sb[:], gt.rearrange("(p t) o -> p (t o)", t=PACK))
+        nc.sync.dma_start(n2_sb[:], n2)
+        nc.sync.dma_start(w1_raw[:].bitcast(I32), w1_words[0].bitcast(I32))
+        for q in range(4):
+            nc.sync.dma_start(w1s_raw[32 * q : 32 * q + 4, :].bitcast(I32), w1_scales[0, 4 * q : 4 * q + 4, :].bitcast(I32))
+        nc.sync.dma_start(tau_sb[:], tau.rearrange("(p t) o -> p (t o)", t=PACK))
+        nc.sync.dma_start(n4_sb[:], n4)
+
+        xs_pick = keep.tile([P, PACK, P], U8, name="xs_pick", align_bytes=64)
+        x_pick = keep.tile([P, PACK, P], U32, name="x_pick", align_bytes=64)
+        nc.vector.tensor_copy(xs_pick[:].rearrange("p t m -> p m t"), xs_all[:].indirect(offs_sb[:]))
+        nc.vector.tensor_copy(x_pick[:].rearrange("p t m -> p m t"), x_all[:].bitcast(U32).indirect(offs_sb[:]))
+
+        wa_codes = []
+        wa_sc = []
+        wa_bf = [keep.tile([P, H // 2, PACK], BF16, name=f"wa_bf{u}", align_bytes=64) for u in range(2)]
+        nc.scalar.activation(wa_bf[0][:].rearrange("p (c i) r -> p c r i", i=4), wa_raw[0][:].rearrange("p r (c i) -> p c r i", i=4), ACT.Copy)
+        nc.vector.tensor_copy(wa_bf[1][:].rearrange("p (c i) r -> p c r i", i=4), wa_raw[1][:].rearrange("p r (c i) -> p c r i", i=4))
+        for u in range(2):
+            codes = keep.tile([P, H // 2], U32, name=f"wa_codes{u}", align_bytes=64)
+            sc = keep.tile([P, H // 2], U8, name=f"wa_sc{u}", align_bytes=64)
+            nc.vector.quantize_mx(out=codes[:].bitcast(FP8X4), scales=sc[:], in_=wa_bf[u][:].rearrange("p c r -> p (c r)"))
+            wa_codes.append(codes)
+            wa_sc.append(sc)
+
+        y = []
+        yg = []
+        for t in range(PACK):
+            bank = psum.tile([P, H], F32, name=f"y_bank{t}")
+            for u in range(2):
+                nc.tensor.matmul_mx(out=bank[:, u * (H // 2) : (u + 1) * (H // 2)], lhsT=x_pick[:, t, :].bitcast(FP8X4), lhsT_scale=xs_pick[:, t, :],
+                                    rhs=wa_codes[u][:].bitcast(FP8X4), rhs_scale=wa_sc[u][:], start=True, stop=True)
+            y_t = keep.tile([P, H], F32, name=f"y{t}")
+            yg_t = keep.tile([P, H], F32, name=f"yg{t}")
+            if t == 1:
+                nc.vector.tensor_copy(y_t[:], bank[:])
+            else:
+                nc.scalar.copy(y_t[:], bank[:])
+            nc.vector.tensor_scalar(yg_t[:], y_t[:], gt_sb[:, t : t + 1], 0.75, ALU.mult, ALU.mult)
+            y.append(y_t)
+            yg.append(yg_t)
+
+        w1_deal = keep.tile([P, PACK, 2 * P], U8, name="w1_deal", align_bytes=64)
+        w1s_deal = keep.tile([P, PACK, P], U8, name="w1s_deal", align_bytes=64)
+        nc.scalar.copy(w1_deal[:].rearrange("p t b -> p (t b)").bitcast(U16).rearrange("p (t m) -> p t m", t=PACK),
+                       w1_raw[:].bitcast(U16).rearrange("p (m t) -> p t m", t=PACK))
+        nc.vector.tensor_copy(w1s_deal[:].rearrange("p t m -> p m t"), w1s_raw[:].rearrange("p (m t) -> p m t", t=PACK))
+
+        h = [keep.tile([P, 2 * H], F32, name=f"h{t}") for t in range(PACK)]
+        h_bank = [psum.tile([P, PACK, CH], F32, name=f"h_bank{c}") for c in range(H // CH)]
+        top = keep.tile([P, PACK, H // CH], F32, name="top")
+        bias = keep.tile([P, PACK], F32, name="bias")
+
+        for j0, width in Z_CHUNKS:
+            cols = slice(j0 // LIST_ROWS, (j0 + width) // LIST_ROWS)
+            u_c = keep.tile([P, PACK, width], F32, name=f"u{j0}")
+            v_c = keep.tile([P, PACK, width], F32, name=f"v{j0}")
+            for t in range(PACK):
+                g1 = h[t][:, H + j0 : H + j0 + width]
+                g3 = ring.tile([P, width], F32, name="g3")
+                nc.scalar.activation(g3[:], y[t][:].indirect(n3_sb[:, cols]), ACT.Copy)
+                nc.scalar.activation(g1, y[t][:].indirect(n1_sb[:, cols]), ACT.Copy)
+                nc.vector.tensor_tensor(v_c[:, t, :], yg[t][:].indirect(n2_sb[:, cols]), g3[:], ALU.mult)
+                nc.vector.tensor_tensor(u_c[:, t, :], yg[t][:, j0 : j0 + width], g1, ALU.mult)
+            z_bf = keep.tile([P, width, PACK], BF16, name=f"z_bf{j0}", align_bytes=64)
+            nc.vector.tensor_tensor(z_bf[:].rearrange("p (c i) t -> p c t i", i=4), u_c[:].rearrange("p t (c i) -> p c t i", i=4),
+                                    v_c[:].rearrange("p t (c i) -> p c t i", i=4), ALU.add)
+            z_codes = keep.tile([P, width], U32, name=f"z_codes{j0}", align_bytes=64)
+            z_sc = keep.tile([P, width], U8, name=f"z_sc{j0}", align_bytes=64)
+            nc.vector.quantize_mx(out=z_codes[:].bitcast(FP8X4), scales=z_sc[:], in_=z_bf[:].rearrange("p c t -> p (c t)"))
+            for k0 in range(0, width, CH):
+                c = (j0 + k0) // CH
+                for t in range(PACK):
+                    nc.tensor.matmul_mx(out=h_bank[c][:, t, :], lhsT=w1_deal[:, t, :].bitcast(FP4X4), lhsT_scale=w1s_deal[:, t, :],
+                                        rhs=z_codes[:, k0 : k0 + CH].bitcast(FP8X4), rhs_scale=z_sc[:, k0 : k0 + CH], start=True, stop=True)
+                for t in range(PACK):
+                    nc.vector.tensor_scalar(h[t][:, c * CH : (c + 1) * CH], h_bank[c][:, t, :], 1.0, None if c == 0 else top[:, t, c - 1 : c],
+                                            ALU.mult, ALU.max, accum_out=top[:, t, c : c + 1])
+                    if c == H // CH - 1:
+                        nc.vector.tensor_scalar(bias[:, t : t + 1], top[:, t, c : c + 1], tau_sb[:, t : t + 1], -1.0, ALU.mult, ALU.mult)
+
+        out_rows = out_0.rearrange("(p t) j -> p t j", t=PACK)
+        out_words = out_1[0].rearrange("p c r -> p (c r)").bitcast(I32)
+        o_sc = keep.tile([P, H], U8, name="o_sc", align_bytes=64)
+        for c in range(H // CH):
+            d_c = keep.tile([P, PACK, CH], F32, name=f"d{c}")
+            o_c = keep.tile([P, PACK, CH], F32, name=f"o{c}")
+            for t in range(PACK):
+                ea = ring.tile([P, CH, 2, 2], F32, name="ea")
+                nc.scalar.activation(ea[:].rearrange("p j a b -> p (j a b)"), h[t][:].indirect(n4_sb[:, c * 32 : (c + 1) * 32]), ACT.Exp,
+                                     bias=bias[:, t : t + 1], scale=tau_sb[:, t : t + 1])
+                hi = ring.tile([P, CH, 2], F32, name="hi")
+                lo = ring.tile([P, CH, 2], F32, name="lo")
+                mx = ring.tile([P, CH], F32, name="mx")
+                mn = ring.tile([P, CH], F32, name="mn")
+                nc.vector.tensor_tensor(hi[:], ea[:, :, 0, :], ea[:, :, 1, :], ALU.max)
+                nc.vector.tensor_tensor(lo[:], ea[:, :, 0, :], ea[:, :, 1, :], ALU.min)
+                nc.vector.tensor_tensor(mx[:], hi[:, :, 0], hi[:, :, 1], ALU.max)
+                nc.vector.tensor_tensor(mn[:], lo[:, :, 0], lo[:, :, 1], ALU.min)
+                nc.vector.tensor_tensor(d_c[:, t, :], mx[:], mn[:], ALU.subtract)
+            nc.vector.scalar_tensor_tensor(o_c[:], d_c[:], 3.0, h_bank[c][:], ALU.mult, ALU.mult)
+            nc.sync.dma_start(out_rows[:, :, c * CH : (c + 1) * CH], o_c[:])
+            o_bf = keep.tile([P, CH, PACK], BF16, name=f"o_bf{c}", align_bytes=64)
+            nc.vector.tensor_copy(o_bf[:].rearrange("p (c i) t -> p c t i", i=4), o_c[:].rearrange("p t (c i) -> p c t i", i=4))
+            o_codes = keep.tile([P, CH], I32, name=f"o_codes{c}", align_bytes=64)
+            nc.vector.quantize_mx(out=o_codes[:].bitcast(FP8X4), scales=o_sc[:, c * CH : (c + 1) * CH], in_=o_bf[:].rearrange("p c t -> p (c t)"))
+            nc.sync.dma_start(out_words[:, c * CH : (c + 1) * CH], o_codes[:])
+        for q in range(4):
+            eng = nc.scalar if q % 2 else nc.sync
+            eng.dma_start(out_2[0, 4 * q : 4 * q + 4, :].bitcast(I32), o_sc[32 * q : 32 * q + 4, :].bitcast(I32))

@@ -20,14 +20,17 @@ P = 128
 PACK = 4
 LIST_ROWS = 16
 CH = 128
-Z_CHUNKS = [(0, 256), (256, 128), (384, 128)]
+Z_CHUNKS = [(0, 384), (384, 128)]
+Z_PARTS = [(0, 256), (256, 128), (384, 128)]
+O_PARTS = [(0, 256), (256, 128), (384, 128)]
+WA_LOADS = [(0, 256), (256, 256)]
+WA_PIECES = [(0, 256), (256, 128), (384, 128)]
 
 
 def tile_picked_tokdotegp_none_po_kernel(tc, x_words, x_scales, wa, gt, w1_words, w1_scales, tau, offs, n1, n2, n3, n4, out_0, out_1, out_2):
     nc = tc.nc
     with ExitStack() as ctx:
         keep = ctx.enter_context(tc.tile_pool(name="keep", bufs=1))
-        ring = ctx.enter_context(tc.tile_pool(name="ring", bufs=3))
         psum = ctx.enter_context(tc.psum_pool(name="psum", bufs=1))
 
         offs_sb = keep.tile([P, S // LIST_ROWS], U16, name="offs_sb")
@@ -37,28 +40,28 @@ def tile_picked_tokdotegp_none_po_kernel(tc, x_words, x_scales, wa, gt, w1_words
         n4_sb = keep.tile([P, W // LIST_ROWS], U16, name="n4_sb")
         x_all = keep.tile([P, T], I32, name="x_all")
         xs_all = keep.tile([P, T], U8, name="xs_all")
-        wa_raw = [keep.tile([P, PACK, H // 2], F32, name=f"wa_raw{u}") for u in range(2)]
+        wa_raw = [keep.tile([P, PACK, width], F32, name=f"wa_raw{j0}") for j0, width in WA_LOADS]
         w1_raw = keep.tile([P, 2 * N], U8, name="w1_raw")
         w1s_raw = keep.tile([P, N], U8, name="w1s_raw")
         gt_sb = keep.tile([P, PACK], F32, name="gt_sb")
         tau_sb = keep.tile([P, PACK], F32, name="tau_sb")
 
-        nc.vector.memset(xs_all[:].bitcast(I32), 0)
-        nc.vector.memset(w1s_raw[:].bitcast(I32), 0)
+        nc.gpsimd.memset(xs_all[:].bitcast(I32), 0)
+        nc.gpsimd.memset(w1s_raw[:].bitcast(I32), 0)
         nc.sync.dma_start(offs_sb[:], offs)
-        nc.sync.dma_start(x_all[:], x_words[0].rearrange("p c r -> p (c r)").bitcast(I32))
         for q in range(4):
-            nc.scalar.dma_start(xs_all[32 * q : 32 * q + 4, :].bitcast(I32), x_scales[0, 4 * q : 4 * q + 4, :].bitcast(I32))
+            nc.sync.dma_start(xs_all[32 * q : 32 * q + 4, :].bitcast(I32), x_scales[0, 4 * q : 4 * q + 4, :].bitcast(I32))
+        nc.sync.dma_start(x_all[:], x_words[0].rearrange("p c r -> p (c r)").bitcast(I32))
         wa_rows = wa.rearrange("(p r) h -> p r h", r=PACK)
-        for u in range(2):
-            nc.sync.dma_start(wa_raw[u][:], wa_rows[:, :, u * (H // 2) : (u + 1) * (H // 2)])
-        nc.sync.dma_start(n3_sb[:], n3)
-        nc.sync.dma_start(n1_sb[:], n1)
-        nc.sync.dma_start(gt_sb[:], gt.rearrange("(p t) o -> p (t o)", t=PACK))
-        nc.sync.dma_start(n2_sb[:], n2)
-        nc.sync.dma_start(w1_raw[:].bitcast(I32), w1_words[0].bitcast(I32))
+        for u, (j0, width) in enumerate(WA_LOADS):
+            nc.sync.dma_start(wa_raw[u][:], wa_rows[:, :, j0 : j0 + width])
+        nc.scalar.dma_start(w1_raw[:].bitcast(I32), w1_words[0].bitcast(I32))
         for q in range(4):
             nc.sync.dma_start(w1s_raw[32 * q : 32 * q + 4, :].bitcast(I32), w1_scales[0, 4 * q : 4 * q + 4, :].bitcast(I32))
+        nc.sync.dma_start(n3_sb[:], n3)
+        nc.sync.dma_start(n1_sb[:], n1)
+        nc.sync.dma_start(n2_sb[:], n2)
+        nc.sync.dma_start(gt_sb[:], gt.rearrange("(p t) o -> p (t o)", t=PACK))
         nc.sync.dma_start(tau_sb[:], tau.rearrange("(p t) o -> p (t o)", t=PACK))
         nc.sync.dma_start(n4_sb[:], n4)
 
@@ -67,100 +70,214 @@ def tile_picked_tokdotegp_none_po_kernel(tc, x_words, x_scales, wa, gt, w1_words
         nc.vector.tensor_copy(xs_pick[:].rearrange("p t m -> p m t"), xs_all[:].indirect(offs_sb[:]))
         nc.vector.tensor_copy(x_pick[:].rearrange("p t m -> p m t"), x_all[:].bitcast(U32).indirect(offs_sb[:]))
 
-        wa_codes = []
-        wa_sc = []
-        wa_bf = [keep.tile([P, H // 2, PACK], BF16, name=f"wa_bf{u}", align_bytes=64) for u in range(2)]
-        nc.scalar.activation(wa_bf[0][:].rearrange("p (c i) r -> p c r i", i=4), wa_raw[0][:].rearrange("p r (c i) -> p c r i", i=4), ACT.Copy)
-        nc.vector.tensor_copy(wa_bf[1][:].rearrange("p (c i) r -> p c r i", i=4), wa_raw[1][:].rearrange("p r (c i) -> p c r i", i=4))
-        for u in range(2):
-            codes = keep.tile([P, H // 2], U32, name=f"wa_codes{u}", align_bytes=64)
-            sc = keep.tile([P, H // 2], U8, name=f"wa_sc{u}", align_bytes=64)
-            nc.vector.quantize_mx(out=codes[:].bitcast(FP8X4), scales=sc[:], in_=wa_bf[u][:].rearrange("p c r -> p (c r)"))
-            wa_codes.append(codes)
-            wa_sc.append(sc)
-
-        y = []
-        yg = []
-        for t in range(PACK):
-            bank = psum.tile([P, H], F32, name=f"y_bank{t}")
-            for u in range(2):
-                nc.tensor.matmul_mx(out=bank[:, u * (H // 2) : (u + 1) * (H // 2)], lhsT=x_pick[:, t, :].bitcast(FP8X4), lhsT_scale=xs_pick[:, t, :],
-                                    rhs=wa_codes[u][:].bitcast(FP8X4), rhs_scale=wa_sc[u][:], start=True, stop=True)
-            y_t = keep.tile([P, H], F32, name=f"y{t}")
-            yg_t = keep.tile([P, H], F32, name=f"yg{t}")
-            if t == 1:
-                nc.vector.tensor_copy(y_t[:], bank[:])
-            else:
-                nc.scalar.copy(y_t[:], bank[:])
-            nc.vector.tensor_scalar(yg_t[:], y_t[:], gt_sb[:, t : t + 1], 0.75, ALU.mult, ALU.mult)
-            y.append(y_t)
-            yg.append(yg_t)
-
         w1_deal = keep.tile([P, PACK, 2 * P], U8, name="w1_deal", align_bytes=64)
         w1s_deal = keep.tile([P, PACK, P], U8, name="w1s_deal", align_bytes=64)
         nc.scalar.copy(w1_deal[:].rearrange("p t b -> p (t b)").bitcast(U16).rearrange("p (t m) -> p t m", t=PACK),
                        w1_raw[:].bitcast(U16).rearrange("p (m t) -> p t m", t=PACK))
+
+        wa_bf = [keep.tile([P, width, PACK], BF16, name=f"wa_bf{j0}", align_bytes=64) for j0, width in WA_PIECES]
+        wa_codes = [keep.tile([P, width], U32, name=f"wa_codes{j0}", align_bytes=64) for j0, width in WA_PIECES]
+        wa_sc = [keep.tile([P, width], U8, name=f"wa_sc{j0}", align_bytes=64) for j0, width in WA_PIECES]
+        for u, (j0, width) in enumerate(WA_PIECES):
+            dst = wa_bf[u][:].rearrange("p (c i) r -> p c r i", i=4)
+            src = wa_raw[j0 // 256][:, :, j0 % 256 : j0 % 256 + width].rearrange("p r (c i) -> p c r i", i=4)
+            if u < 2:
+                nc.scalar.activation(dst, src, ACT.Copy)
+            else:
+                nc.vector.tensor_copy(dst, src)
+        for u in (0, 2, 1):
+            nc.vector.quantize_mx(out=wa_codes[u][:].bitcast(FP8X4), scales=wa_sc[u][:], in_=wa_bf[u][:].rearrange("p c r -> p (c r)"))
         nc.vector.tensor_copy(w1s_deal[:].rearrange("p t m -> p m t"), w1s_raw[:].rearrange("p (m t) -> p m t", t=PACK))
 
-        h = [keep.tile([P, 2 * H], F32, name=f"h{t}") for t in range(PACK)]
-        h_bank = [psum.tile([P, PACK, CH], F32, name=f"h_bank{c}") for c in range(H // CH)]
-        top = keep.tile([P, PACK, H // CH], F32, name="top")
-        bias = keep.tile([P, PACK], F32, name="bias")
+        y_bank = [psum.tile([P, H], F32, name=f"y_bank{t}") for t in range(PACK)]
+        for t in range(PACK):
+            for u, (j0, width) in enumerate(WA_PIECES):
+                nc.tensor.matmul_mx(out=y_bank[t][:, j0 : j0 + width], lhsT=x_pick[:, t, :].bitcast(FP8X4), lhsT_scale=xs_pick[:, t, :],
+                                    rhs=wa_codes[u][:].bitcast(FP8X4), rhs_scale=wa_sc[u][:], start=True, stop=True)
 
-        for j0, width in Z_CHUNKS:
-            cols = slice(j0 // LIST_ROWS, (j0 + width) // LIST_ROWS)
-            u_c = keep.tile([P, PACK, width], F32, name=f"u{j0}")
-            v_c = keep.tile([P, PACK, width], F32, name=f"v{j0}")
-            for t in range(PACK):
-                g1 = h[t][:, H + j0 : H + j0 + width]
-                g3 = ring.tile([P, width], F32, name="g3")
-                nc.scalar.activation(g3[:], y[t][:].indirect(n3_sb[:, cols]), ACT.Copy)
-                nc.scalar.activation(g1, y[t][:].indirect(n1_sb[:, cols]), ACT.Copy)
-                nc.vector.tensor_tensor(v_c[:, t, :], yg[t][:].indirect(n2_sb[:, cols]), g3[:], ALU.mult)
-                nc.vector.tensor_tensor(u_c[:, t, :], yg[t][:, j0 : j0 + width], g1, ALU.mult)
-            z_bf = keep.tile([P, width, PACK], BF16, name=f"z_bf{j0}", align_bytes=64)
-            nc.vector.tensor_tensor(z_bf[:].rearrange("p (c i) t -> p c t i", i=4), u_c[:].rearrange("p t (c i) -> p c t i", i=4),
-                                    v_c[:].rearrange("p t (c i) -> p c t i", i=4), ALU.add)
-            z_codes = keep.tile([P, width], U32, name=f"z_codes{j0}", align_bytes=64)
-            z_sc = keep.tile([P, width], U8, name=f"z_sc{j0}", align_bytes=64)
-            nc.vector.quantize_mx(out=z_codes[:].bitcast(FP8X4), scales=z_sc[:], in_=z_bf[:].rearrange("p c t -> p (c t)"))
-            for k0 in range(0, width, CH):
-                c = (j0 + k0) // CH
-                for t in range(PACK):
-                    nc.tensor.matmul_mx(out=h_bank[c][:, t, :], lhsT=w1_deal[:, t, :].bitcast(FP4X4), lhsT_scale=w1s_deal[:, t, :],
-                                        rhs=z_codes[:, k0 : k0 + CH].bitcast(FP8X4), rhs_scale=z_sc[:, k0 : k0 + CH], start=True, stop=True)
-                for t in range(PACK):
-                    nc.vector.tensor_scalar(h[t][:, c * CH : (c + 1) * CH], h_bank[c][:, t, :], 1.0, None if c == 0 else top[:, t, c - 1 : c],
-                                            ALU.mult, ALU.max, accum_out=top[:, t, c : c + 1])
-                    if c == H // CH - 1:
-                        nc.vector.tensor_scalar(bias[:, t : t + 1], top[:, t, c : c + 1], tau_sb[:, t : t + 1], -1.0, ALU.mult, ALU.mult)
+        y = [keep.tile([P, H], F32, name=f"y{t}") for t in range(PACK)]
+        gw = keep.tile([P, PACK], F32, name="gw")
+        nc.vector.tensor_scalar(gw[:], gt_sb[:], 0.75, None, ALU.mult)
+        h = [keep.tile([P, 2 * H], F32, name=f"h{t}") for t in range(PACK)]
+        h_bank = [psum.tile([P, H], F32, name=f"h_bank{t}") for t in range(PACK)]
+        early = keep.tile([P, 1], F32, name="early")
+        top = keep.tile([P, PACK], F32, name="top")
+        bias = keep.tile([P, PACK], F32, name="bias")
+        g1 = [keep.tile([P, PACK, width], F32, name=f"g1{j0}") for j0, width in Z_CHUNKS]
+        u_c = [keep.tile([P, PACK, width], F32, name=f"u{j0}") for j0, width in Z_CHUNKS]
+        v_c = [keep.tile([P, PACK, width], F32, name=f"v{j0}") for j0, width in Z_CHUNKS]
+        z = keep.tile([P, PACK, H], BF16, name="z")
+        z_bf = [keep.tile([P, width, PACK], BF16, name=f"z_bf{j0}", align_bytes=64) for j0, width in Z_PARTS]
+        z_codes = keep.tile([P, H], U32, name="z_codes", align_bytes=64)
+        z_sc = keep.tile([P, H], U8, name="z_sc", align_bytes=64)
+
+        def entries(lst, k):
+            j0, width = Z_CHUNKS[k]
+            return lst[:, j0 // LIST_ROWS : (j0 + width) // LIST_ROWS]
+
+        def g3(k, t):
+            j0, width = Z_CHUNKS[k]
+            return h[t][:, H + j0 : H + j0 + width]
+
+        def fetch1(k, t):
+            nc.scalar.activation(g1[k][:, t, :], y[t][:].indirect(entries(n1_sb, k)), ACT.Copy)
+
+        def fetch3(k, t):
+            nc.scalar.activation(g3(k, t), y[t][:].indirect(entries(n3_sb, k)), ACT.Copy)
+
+        def second_term(k, t):
+            nc.vector.tensor_tensor(v_c[k][:, t, :], y[t][:].indirect(entries(n2_sb, k)), g3(k, t), ALU.mult)
+
+        def first_term(k, t):
+            j0, width = Z_CHUNKS[k]
+            nc.vector.scalar_tensor_tensor(u_c[k][:, t, :], g1[k][:, t, :], gw[:, t : t + 1], y[t][:, j0 : j0 + width], ALU.mult, ALU.mult)
+
+        def summed(k, t):
+            j0, width = Z_CHUNKS[k]
+            nc.vector.scalar_tensor_tensor(z[:, t, j0 : j0 + width], v_c[k][:, t, :], gw[:, t : t + 1], u_c[k][:, t, :], ALU.mult, ALU.add)
+
+        def woven(k, on_scalar):
+            j0, width = Z_PARTS[k]
+            dst = z_bf[k][:].rearrange("p (c i) t -> p c t i", i=4)
+            src = z[:, :, j0 : j0 + width].rearrange("p t (c i) -> p c t i", i=4)
+            if on_scalar:
+                nc.scalar.copy(dst, src)
+            else:
+                nc.vector.tensor_copy(dst, src)
+
+        def quantised(k):
+            j0, width = Z_PARTS[k]
+            nc.vector.quantize_mx(out=z_codes[:, j0 : j0 + width].bitcast(FP8X4), scales=z_sc[:, j0 : j0 + width], in_=z_bf[k][:].rearrange("p c t -> p (c t)"))
+
+        def second_product(t, cols):
+            nc.tensor.matmul_mx(out=h_bank[t][:, cols], lhsT=w1_deal[:, t, :].bitcast(FP4X4), lhsT_scale=w1s_deal[:, t, :],
+                                rhs=z_codes[:, cols].bitcast(FP8X4), rhs_scale=z_sc[:, cols], start=True, stop=True)
+
+        def bring_h(t, cols, so_far, largest):
+            nc.vector.tensor_scalar(h[t][:, cols], h_bank[t][:, cols], 1.0, so_far, ALU.mult, ALU.max, accum_out=largest)
+
+        def make_bias(t):
+            nc.vector.tensor_scalar(bias[:, t : t + 1], top[:, t : t + 1], tau_sb[:, t : t + 1], -1.0, ALU.mult, ALU.mult)
 
         out_rows = out_0.rearrange("(p t) j -> p t j", t=PACK)
         out_words = out_1[0].rearrange("p c r -> p (c r)").bitcast(I32)
         o_sc = keep.tile([P, H], U8, name="o_sc", align_bytes=64)
-        for c in range(H // CH):
-            d_c = keep.tile([P, PACK, CH], F32, name=f"d{c}")
-            o_c = keep.tile([P, PACK, CH], F32, name=f"o{c}")
-            for t in range(PACK):
-                ea = ring.tile([P, CH, 2, 2], F32, name="ea")
-                nc.scalar.activation(ea[:].rearrange("p j a b -> p (j a b)"), h[t][:].indirect(n4_sb[:, c * 32 : (c + 1) * 32]), ACT.Exp,
-                                     bias=bias[:, t : t + 1], scale=tau_sb[:, t : t + 1])
-                hi = ring.tile([P, CH, 2], F32, name="hi")
-                lo = ring.tile([P, CH, 2], F32, name="lo")
-                mx = ring.tile([P, CH], F32, name="mx")
-                mn = ring.tile([P, CH], F32, name="mn")
-                nc.vector.tensor_tensor(hi[:], ea[:, :, 0, :], ea[:, :, 1, :], ALU.max)
-                nc.vector.tensor_tensor(lo[:], ea[:, :, 0, :], ea[:, :, 1, :], ALU.min)
-                nc.vector.tensor_tensor(mx[:], hi[:, :, 0], hi[:, :, 1], ALU.max)
-                nc.vector.tensor_tensor(mn[:], lo[:, :, 0], lo[:, :, 1], ALU.min)
-                nc.vector.tensor_tensor(d_c[:, t, :], mx[:], mn[:], ALU.subtract)
-            nc.vector.scalar_tensor_tensor(o_c[:], d_c[:], 3.0, h_bank[c][:], ALU.mult, ALU.mult)
-            nc.sync.dma_start(out_rows[:, :, c * CH : (c + 1) * CH], o_c[:])
-            o_bf = keep.tile([P, CH, PACK], BF16, name=f"o_bf{c}", align_bytes=64)
-            nc.vector.tensor_copy(o_bf[:].rearrange("p (c i) t -> p c t i", i=4), o_c[:].rearrange("p t (c i) -> p c t i", i=4))
-            o_codes = keep.tile([P, CH], I32, name=f"o_codes{c}", align_bytes=64)
-            nc.vector.quantize_mx(out=o_codes[:].bitcast(FP8X4), scales=o_sc[:, c * CH : (c + 1) * CH], in_=o_bf[:].rearrange("p c t -> p (c t)"))
-            nc.sync.dma_start(out_words[:, c * CH : (c + 1) * CH], o_codes[:])
+        n_ch = H // CH
+        ea = [[keep.tile([P, CH, 2, 2], F32, name=f"ea{c}_{t}") for t in range(PACK)] for c in range(n_ch)]
+        hi = [keep.tile([P, H, 2], F32, name=f"hi{t}") for t in range(PACK)]
+        lo = [keep.tile([P, H, 2], F32, name=f"lo{t}") for t in range(PACK)]
+        mx = [keep.tile([P, H], F32, name=f"mx{t}") for t in range(PACK)]
+        mn = [keep.tile([P, H], F32, name=f"mn{t}") for t in range(PACK)]
+        d = [keep.tile([P, H], F32, name=f"d{t}") for t in range(PACK)]
+        o = keep.tile([P, PACK, H], F32, name="o")
+        o_bf = [keep.tile([P, width, PACK], BF16, name=f"o_bf{j0}", align_bytes=64) for j0, width in O_PARTS]
+        o_codes = [keep.tile([P, width], I32, name=f"o_codes{j0}", align_bytes=64) for j0, width in O_PARTS]
+
+        def span(c0, c1):
+            return slice(c0 * CH, c1 * CH)
+
+        def fetch4(c, t):
+            nc.scalar.activation(ea[c][t][:].rearrange("p j a b -> p (j a b)"), h[t][:].indirect(n4_sb[:, c * 32 : (c + 1) * 32]), ACT.Exp,
+                                 bias=bias[:, t : t + 1], scale=tau_sb[:, t : t + 1])
+
+        def pair_hi(c, t):
+            nc.vector.tensor_tensor(hi[t][:, span(c, c + 1), :], ea[c][t][:, :, 0, :], ea[c][t][:, :, 1, :], ALU.max)
+
+        def pair_lo(c, t):
+            nc.vector.tensor_tensor(lo[t][:, span(c, c + 1), :], ea[c][t][:, :, 0, :], ea[c][t][:, :, 1, :], ALU.min)
+
+        def ends(t, cols):
+            nc.vector.tensor_tensor(mx[t][:, cols], hi[t][:, cols, 0], hi[t][:, cols, 1], ALU.max)
+            nc.vector.tensor_tensor(mn[t][:, cols], lo[t][:, cols, 0], lo[t][:, cols, 1], ALU.min)
+
+        def spread(t, cols):
+            nc.vector.tensor_tensor(d[t][:, cols], mx[t][:, cols], mn[t][:, cols], ALU.subtract)
+
+        def result(t, cols):
+            nc.vector.scalar_tensor_tensor(o[:, t, cols], d[t][:, cols], 3.0, h_bank[t][:, cols], ALU.mult, ALU.mult)
+
+        def store(ts, cols):
+            nc.sync.dma_start(out_rows[:, ts, cols], o[:, ts, cols])
+
+        def rounded(k, on_scalar):
+            j0, width = O_PARTS[k]
+            dst = o_bf[k][:].rearrange("p (c i) t -> p c t i", i=4)
+            src = o[:, :, j0 : j0 + width].rearrange("p t (c i) -> p c t i", i=4)
+            if on_scalar:
+                nc.scalar.copy(dst, src)
+            else:
+                nc.vector.tensor_copy(dst, src)
+
+        def planes(k):
+            j0, width = O_PARTS[k]
+            nc.vector.quantize_mx(out=o_codes[k][:].bitcast(FP8X4), scales=o_sc[:, j0 : j0 + width], in_=o_bf[k][:].rearrange("p c t -> p (c t)"))
+            nc.sync.dma_start(out_words[:, j0 : j0 + width], o_codes[k][:])
+
+        nc.scalar.copy(y[0][:], y_bank[0][:])
+        for t in range(1, PACK):
+            nc.vector.tensor_copy(y[t][:], y_bank[t][:])
+        steps = [(k, t) for k in range(len(Z_CHUNKS)) for t in range(PACK)]
+        for n, (k, t) in enumerate(steps):
+            fetch3(k, t)
+            fetch1(k, t)
+            second_term(k, t)
+            if n > 0:
+                summed(*steps[n - 1])
+            first_term(k, t)
+        woven(0, True)
+        woven(1, True)
+        quantised(0)
+        summed(*steps[-1])
+        second_product(0, slice(0, 256))
+        woven(2, False)
+        quantised(1)
+        quantised(2)
+        bring_h(0, slice(0, 256), None, early[:])
+        second_product(0, slice(256, H))
+        bring_h(0, slice(256, H), early[:], top[:, 0:1])
+        make_bias(0)
+        for t in range(1, PACK):
+            second_product(t, slice(0, H))
+            bring_h(t, slice(0, H), None, top[:, t : t + 1])
+            make_bias(t)
+        units = [(c0, t) for t in range(PACK) for c0 in (0, 2)]
+        for c0, t in units:
+            fetch4(c0, t)
+            fetch4(c0 + 1, t)
+        before = None
+        for c0, t in units[:-1]:
+            pair_hi(c0, t)
+            if before:
+                spread(*before)
+            pair_lo(c0, t)
+            if before:
+                result(*before)
+                store(slice(before[0], before[0] + 1), before[1])
+            pair_hi(c0 + 1, t)
+            pair_lo(c0 + 1, t)
+            before = (t, span(c0, c0 + 2))
+            ends(*before)
+        last = PACK - 1
+        pair_hi(2, last)
+        spread(*before)
+        pair_lo(2, last)
+        result(*before)
+        store(slice(before[0], before[0] + 1), before[1])
+        ends(last, span(2, 3))
+        rounded(0, True)
+        pair_hi(3, last)
+        spread(last, span(2, 3))
+        pair_lo(3, last)
+        result(last, span(2, 3))
+        rounded(1, True)
+        ends(last, span(3, 4))
+        planes(0)
+        spread(last, span(3, 4))
+        result(last, span(3, 4))
+        store(slice(last, last + 1), span(2, 4))
+        rounded(2, False)
+        planes(1)
+        planes(2)
         for q in range(4):
             eng = nc.scalar if q % 2 else nc.sync
             eng.dma_start(out_2[0, 4 * q : 4 * q + 4, :].bitcast(I32), o_sc[32 * q : 32 * q + 4, :].bitcast(I32))

@@ -21,6 +21,7 @@ PACK = 4
 LIST_ROWS = 16
 CH = 128
 Z_CHUNKS = [(0, 384), (384, 128)]
+TOPCOL = (0, 0, 2, 3)
 Z_PARTS = [(0, 256), (256, 128), (384, 128)]
 O_PARTS = [(0, 256), (256, 128), (384, 128)]
 WA_LOADS = [(0, 256), (256, 256)]
@@ -46,7 +47,7 @@ def tile_picked_tokdotegp_none_po_kernel(tc, x_words, x_scales, wa, gt, w1_words
         gt_sb = keep.tile([P, PACK], F32, name="gt_sb")
         tau_sb = keep.tile([P, PACK], F32, name="tau_sb")
 
-        nc.gpsimd.memset(xs_all[:].bitcast(I32), 0)
+        nc.vector.memset(xs_all[:].bitcast(I32), 0)
         nc.gpsimd.memset(w1s_raw[:].bitcast(I32), 0)
         nc.sync.dma_start(offs_sb[:], offs)
         for q in range(4):
@@ -96,12 +97,11 @@ def tile_picked_tokdotegp_none_po_kernel(tc, x_words, x_scales, wa, gt, w1_words
                                     rhs=wa_codes[u][:].bitcast(FP8X4), rhs_scale=wa_sc[u][:], start=True, stop=True)
 
         y = [keep.tile([P, H], F32, name=f"y{t}") for t in range(PACK)]
-        gw = keep.tile([P, PACK], F32, name="gw")
-        nc.vector.tensor_scalar(gw[:], gt_sb[:], 0.75, None, ALU.mult)
         h = [keep.tile([P, 2 * H], F32, name=f"h{t}") for t in range(PACK)]
         h_bank = [psum.tile([P, H], F32, name=f"h_bank{t}") for t in range(PACK)]
         early = keep.tile([P, 1], F32, name="early")
-        top = keep.tile([P, PACK], F32, name="top")
+        tops = keep.tile([P, PACK], F32, name="tops")
+        top = [tops[:, c : c + 1] for c in TOPCOL]
         bias = keep.tile([P, PACK], F32, name="bias")
         g1 = [keep.tile([P, PACK, width], F32, name=f"g1{j0}") for j0, width in Z_CHUNKS]
         u_c = [keep.tile([P, PACK, width], F32, name=f"u{j0}") for j0, width in Z_CHUNKS]
@@ -120,21 +120,21 @@ def tile_picked_tokdotegp_none_po_kernel(tc, x_words, x_scales, wa, gt, w1_words
             return h[t][:, H + j0 : H + j0 + width]
 
         def fetch1(k, t):
-            nc.scalar.activation(g1[k][:, t, :], y[t][:].indirect(entries(n1_sb, k)), ACT.Copy)
+            nc.scalar.activation(g1[k][:, t, :], y[t][:].indirect(entries(n1_sb, k)), ACT.Copy, scale=0.75)
 
         def fetch3(k, t):
-            nc.scalar.activation(g3(k, t), y[t][:].indirect(entries(n3_sb, k)), ACT.Copy)
+            nc.scalar.activation(g3(k, t), y[t][:].indirect(entries(n3_sb, k)), ACT.Copy, scale=0.75)
 
         def second_term(k, t):
             nc.vector.tensor_tensor(v_c[k][:, t, :], y[t][:].indirect(entries(n2_sb, k)), g3(k, t), ALU.mult)
 
         def first_term(k, t):
             j0, width = Z_CHUNKS[k]
-            nc.vector.scalar_tensor_tensor(u_c[k][:, t, :], g1[k][:, t, :], gw[:, t : t + 1], y[t][:, j0 : j0 + width], ALU.mult, ALU.mult)
+            nc.vector.scalar_tensor_tensor(u_c[k][:, t, :], g1[k][:, t, :], gt_sb[:, t : t + 1], y[t][:, j0 : j0 + width], ALU.mult, ALU.mult)
 
         def summed(k, t):
             j0, width = Z_CHUNKS[k]
-            nc.vector.scalar_tensor_tensor(z[:, t, j0 : j0 + width], v_c[k][:, t, :], gw[:, t : t + 1], u_c[k][:, t, :], ALU.mult, ALU.add)
+            nc.vector.scalar_tensor_tensor(z[:, t, j0 : j0 + width], v_c[k][:, t, :], gt_sb[:, t : t + 1], u_c[k][:, t, :], ALU.mult, ALU.add)
 
         def woven(k, on_scalar):
             j0, width = Z_PARTS[k]
@@ -157,7 +157,7 @@ def tile_picked_tokdotegp_none_po_kernel(tc, x_words, x_scales, wa, gt, w1_words
             nc.vector.tensor_scalar(h[t][:, cols], h_bank[t][:, cols], 1.0, so_far, ALU.mult, ALU.max, accum_out=largest)
 
         def make_bias(t):
-            nc.vector.tensor_scalar(bias[:, t : t + 1], top[:, t : t + 1], tau_sb[:, t : t + 1], -1.0, ALU.mult, ALU.mult)
+            nc.vector.tensor_scalar(bias[:, t : t + 1], top[t], tau_sb[:, t : t + 1], -1.0, ALU.mult, ALU.mult)
 
         out_rows = out_0.rearrange("(p t) j -> p t j", t=PACK)
         out_words = out_1[0].rearrange("p c r -> p (c r)").bitcast(I32)
@@ -186,8 +186,10 @@ def tile_picked_tokdotegp_none_po_kernel(tc, x_words, x_scales, wa, gt, w1_words
         def pair_lo(c, t):
             nc.vector.tensor_tensor(lo[t][:, span(c, c + 1), :], ea[c][t][:, :, 0, :], ea[c][t][:, :, 1, :], ALU.min)
 
-        def ends(t, cols):
+        def largest(t, cols):
             nc.vector.tensor_tensor(mx[t][:, cols], hi[t][:, cols, 0], hi[t][:, cols, 1], ALU.max)
+
+        def smallest(t, cols):
             nc.vector.tensor_tensor(mn[t][:, cols], lo[t][:, cols, 0], lo[t][:, cols, 1], ALU.min)
 
         def spread(t, cols):
@@ -234,11 +236,11 @@ def tile_picked_tokdotegp_none_po_kernel(tc, x_words, x_scales, wa, gt, w1_words
         quantised(2)
         bring_h(0, slice(0, 256), None, early[:])
         second_product(0, slice(256, H))
-        bring_h(0, slice(256, H), early[:], top[:, 0:1])
+        bring_h(0, slice(256, H), early[:], top[0])
         make_bias(0)
         for t in range(1, PACK):
             second_product(t, slice(0, H))
-            bring_h(t, slice(0, H), None, top[:, t : t + 1])
+            bring_h(t, slice(0, H), None, top[t])
             make_bias(t)
         units = [(c0, t) for t in range(PACK) for c0 in (0, 2)]
         for c0, t in units:
@@ -256,27 +258,30 @@ def tile_picked_tokdotegp_none_po_kernel(tc, x_words, x_scales, wa, gt, w1_words
             pair_hi(c0 + 1, t)
             pair_lo(c0 + 1, t)
             before = (t, span(c0, c0 + 2))
-            ends(*before)
+            largest(*before)
+            smallest(*before)
         last = PACK - 1
         pair_hi(2, last)
         spread(*before)
         pair_lo(2, last)
         result(*before)
         store(slice(before[0], before[0] + 1), before[1])
-        ends(last, span(2, 3))
         rounded(0, True)
         pair_hi(3, last)
-        spread(last, span(2, 3))
+        largest(last, span(2, 3))
+        smallest(last, span(2, 3))
         pair_lo(3, last)
+        spread(last, span(2, 3))
+        largest(last, span(3, 4))
         result(last, span(2, 3))
         rounded(1, True)
-        ends(last, span(3, 4))
+        smallest(last, span(3, 4))
         planes(0)
         spread(last, span(3, 4))
         result(last, span(3, 4))
         store(slice(last, last + 1), span(2, 4))
-        rounded(2, False)
         planes(1)
+        rounded(2, False)
         planes(2)
         for q in range(4):
             eng = nc.scalar if q % 2 else nc.sync

@@ -18,21 +18,38 @@ ACT = mybir.ActivationFunctionType
 
 P = 128
 PACK = 4
+QUADS = 4
 LIST_ROWS = 16
-CH = 128
-Z_CHUNKS = [(0, 384), (384, 128)]
-TOPCOL = (0, 0, 2, 3)
-Z_PARTS = [(0, 256), (256, 128), (384, 128)]
-O_PARTS = [(0, 256), (256, 128), (384, 128)]
-WA_LOADS = [(0, 256), (256, 256)]
-WA_PIECES = [(0, 256), (256, 128), (384, 128)]
+MEMBERS = W // H
+RUN = 4
+HALF = H // 2
+STEP = 128
+LAST = PACK - 1
+
+WA_LOADS = [(0, HALF), (HALF, HALF)]
+PARTS = [(0, HALF), (HALF, STEP), (HALF + STEP, STEP)]
+Z_CHUNKS = [(0, H - STEP), (H - STEP, STEP)]
 
 
-def tile_picked_tokdotegp_none_po_kernel(tc, x_words, x_scales, wa, gt, w1_words, w1_scales, tau, offs, n1, n2, n3, n4, out_0, out_1, out_2):
+def tile_picked_tokdotegp_none_po_kernel(
+    tc, x_words, x_scales, wa, gt, w1_words, w1_scales, tau, offs, n1, n2, n3, n4, out_0, out_1, out_2
+):
     nc = tc.nc
     with ExitStack() as ctx:
         keep = ctx.enter_context(tc.tile_pool(name="keep", bufs=1))
         psum = ctx.enter_context(tc.psum_pool(name="psum", bufs=1))
+
+        def weave(copy, woven_tile, row_sets):
+            copy(woven_tile[:].rearrange("p (c i) t -> p c t i", i=RUN), row_sets.rearrange("p t (c i) -> p c t i", i=RUN))
+
+        def scalar_cast(out, in_):
+            nc.scalar.activation(out, in_, ACT.Copy)
+
+        def quantise(codes, scales, woven_tile):
+            nc.vector.quantize_mx(out=codes.bitcast(FP8X4), scales=scales, in_=woven_tile[:].rearrange("p j t -> p (j t)"))
+
+        def cols_of(part):
+            return slice(part[0], part[0] + part[1])
 
         offs_sb = keep.tile([P, S // LIST_ROWS], U16, name="offs_sb")
         n1_sb = keep.tile([P, H // LIST_ROWS], U16, name="n1_sb")
@@ -47,22 +64,24 @@ def tile_picked_tokdotegp_none_po_kernel(tc, x_words, x_scales, wa, gt, w1_words
         gt_sb = keep.tile([P, PACK], F32, name="gt_sb")
         tau_sb = keep.tile([P, PACK], F32, name="tau_sb")
 
+        def load_scale_rows(tile, scales):
+            for q in range(QUADS):
+                nc.sync.dma_start(tile[32 * q : 32 * q + 4, :].bitcast(I32), scales[0, 4 * q : 4 * q + 4, :].bitcast(I32))
+
         nc.vector.memset(xs_all[:].bitcast(I32), 0)
         nc.gpsimd.memset(w1s_raw[:].bitcast(I32), 0)
         nc.sync.dma_start(offs_sb[:], offs)
-        for q in range(4):
-            nc.sync.dma_start(xs_all[32 * q : 32 * q + 4, :].bitcast(I32), x_scales[0, 4 * q : 4 * q + 4, :].bitcast(I32))
-        nc.sync.dma_start(x_all[:], x_words[0].rearrange("p c r -> p (c r)").bitcast(I32))
+        load_scale_rows(xs_all, x_scales)
         wa_rows = wa.rearrange("(p r) h -> p r h", r=PACK)
-        for u, (j0, width) in enumerate(WA_LOADS):
-            nc.sync.dma_start(wa_raw[u][:], wa_rows[:, :, j0 : j0 + width])
-        nc.scalar.dma_start(w1_raw[:].bitcast(I32), w1_words[0].bitcast(I32))
-        for q in range(4):
-            nc.sync.dma_start(w1s_raw[32 * q : 32 * q + 4, :].bitcast(I32), w1_scales[0, 4 * q : 4 * q + 4, :].bitcast(I32))
+        nc.sync.dma_start(wa_raw[0][:], wa_rows[:, :, cols_of(WA_LOADS[0])])
         nc.sync.dma_start(n3_sb[:], n3)
+        nc.sync.dma_start(x_all[:], x_words[0].rearrange("p c r -> p (c r)").bitcast(I32))
+        nc.sync.dma_start(wa_raw[1][:], wa_rows[:, :, cols_of(WA_LOADS[1])])
+        nc.sync.dma_start(w1_raw[:].bitcast(I32), w1_words[0].bitcast(I32))
         nc.sync.dma_start(n1_sb[:], n1)
         nc.sync.dma_start(n2_sb[:], n2)
         nc.sync.dma_start(gt_sb[:], gt.rearrange("(p t) o -> p (t o)", t=PACK))
+        load_scale_rows(w1s_raw, w1_scales)
         nc.sync.dma_start(tau_sb[:], tau.rearrange("(p t) o -> p (t o)", t=PACK))
         nc.sync.dma_start(n4_sb[:], n4)
 
@@ -73,88 +92,87 @@ def tile_picked_tokdotegp_none_po_kernel(tc, x_words, x_scales, wa, gt, w1_words
 
         w1_deal = keep.tile([P, PACK, 2 * P], U8, name="w1_deal", align_bytes=64)
         w1s_deal = keep.tile([P, PACK, P], U8, name="w1s_deal", align_bytes=64)
-        nc.scalar.copy(w1_deal[:].rearrange("p t b -> p (t b)").bitcast(U16).rearrange("p (t m) -> p t m", t=PACK),
-                       w1_raw[:].bitcast(U16).rearrange("p (m t) -> p t m", t=PACK))
 
-        wa_bf = [keep.tile([P, width, PACK], BF16, name=f"wa_bf{j0}", align_bytes=64) for j0, width in WA_PIECES]
-        wa_codes = [keep.tile([P, width], U32, name=f"wa_codes{j0}", align_bytes=64) for j0, width in WA_PIECES]
-        wa_sc = [keep.tile([P, width], U8, name=f"wa_sc{j0}", align_bytes=64) for j0, width in WA_PIECES]
-        for u, (j0, width) in enumerate(WA_PIECES):
-            dst = wa_bf[u][:].rearrange("p (c i) r -> p c r i", i=4)
-            src = wa_raw[j0 // 256][:, :, j0 % 256 : j0 % 256 + width].rearrange("p r (c i) -> p c r i", i=4)
-            if u < 2:
-                nc.scalar.activation(dst, src, ACT.Copy)
-            else:
-                nc.vector.tensor_copy(dst, src)
-        for u in (0, 2, 1):
-            nc.vector.quantize_mx(out=wa_codes[u][:].bitcast(FP8X4), scales=wa_sc[u][:], in_=wa_bf[u][:].rearrange("p c r -> p (c r)"))
+        wa_bf = [keep.tile([P, width, PACK], BF16, name=f"wa_bf{j0}", align_bytes=64) for j0, width in PARTS]
+        wa_codes = keep.tile([P, H], U32, name="wa_codes", align_bytes=64)
+        wa_sc = keep.tile([P, H], U8, name="wa_sc", align_bytes=64)
+        weave(scalar_cast, wa_bf[0], wa_raw[0][:])
+        weave(scalar_cast, wa_bf[1], wa_raw[1][:, :, :STEP])
+        weave(nc.vector.tensor_copy, wa_bf[2], wa_raw[1][:, :, STEP:])
+        for k in (0, 2, 1):
+            quantise(wa_codes[:, cols_of(PARTS[k])], wa_sc[:, cols_of(PARTS[k])], wa_bf[k])
+
+        nc.scalar.copy(
+            w1_deal[:].rearrange("p t b -> p (t b)").bitcast(U16).rearrange("p (t m) -> p t m", t=PACK),
+            w1_raw[:].bitcast(U16).rearrange("p (m t) -> p t m", t=PACK),
+        )
         nc.vector.tensor_copy(w1s_deal[:].rearrange("p t m -> p m t"), w1s_raw[:].rearrange("p (m t) -> p m t", t=PACK))
 
+        whole_row = slice(0, H)
+        first_half, second_half = slice(0, HALF), slice(HALF, H)
         y_bank = [psum.tile([P, H], F32, name=f"y_bank{t}") for t in range(PACK)]
         for t in range(PACK):
-            for u, (j0, width) in enumerate(WA_PIECES):
-                nc.tensor.matmul_mx(out=y_bank[t][:, j0 : j0 + width], lhsT=x_pick[:, t, :].bitcast(FP8X4), lhsT_scale=xs_pick[:, t, :],
-                                    rhs=wa_codes[u][:].bitcast(FP8X4), rhs_scale=wa_sc[u][:], start=True, stop=True)
+            for cols in [first_half, second_half] if t == 0 else [whole_row]:
+                nc.tensor.matmul_mx(
+                    out=y_bank[t][:, cols], lhsT=x_pick[:, t, :].bitcast(FP8X4), lhsT_scale=xs_pick[:, t, :],
+                    rhs=wa_codes[:, cols].bitcast(FP8X4), rhs_scale=wa_sc[:, cols], start=True, stop=True,
+                )
 
         y = [keep.tile([P, H], F32, name=f"y{t}") for t in range(PACK)]
         h = [keep.tile([P, 2 * H], F32, name=f"h{t}") for t in range(PACK)]
         h_bank = [psum.tile([P, H], F32, name=f"h_bank{t}") for t in range(PACK)]
-        early = keep.tile([P, 1], F32, name="early")
-        tops = keep.tile([P, PACK], F32, name="tops")
-        top = [tops[:, c : c + 1] for c in TOPCOL]
+        top_first_half = keep.tile([P, 1], F32, name="top_first_half")
+        tops = keep.tile([P, LAST], F32, name="tops")
+        top = [tops[:, max(t - 1, 0) : max(t - 1, 0) + 1] for t in range(PACK)]
         bias = keep.tile([P, PACK], F32, name="bias")
-        g1 = [keep.tile([P, PACK, width], F32, name=f"g1{j0}") for j0, width in Z_CHUNKS]
-        u_c = [keep.tile([P, PACK, width], F32, name=f"u{j0}") for j0, width in Z_CHUNKS]
-        v_c = [keep.tile([P, PACK, width], F32, name=f"v{j0}") for j0, width in Z_CHUNKS]
+        y_n1 = [keep.tile([P, PACK, width], F32, name=f"y_n1_{j0}") for j0, width in Z_CHUNKS]
+        term_a = [keep.tile([P, PACK, width], F32, name=f"term_a{j0}") for j0, width in Z_CHUNKS]
+        term_b = [keep.tile([P, PACK, width], F32, name=f"term_b{j0}") for j0, width in Z_CHUNKS]
         z = keep.tile([P, PACK, H], BF16, name="z")
-        z_bf = [keep.tile([P, width, PACK], BF16, name=f"z_bf{j0}", align_bytes=64) for j0, width in Z_PARTS]
+        z_bf = [keep.tile([P, width, PACK], BF16, name=f"z_bf{j0}", align_bytes=64) for j0, width in PARTS]
         z_codes = keep.tile([P, H], U32, name="z_codes", align_bytes=64)
         z_sc = keep.tile([P, H], U8, name="z_sc", align_bytes=64)
 
-        def entries(lst, k):
-            j0, width = Z_CHUNKS[k]
-            return lst[:, j0 // LIST_ROWS : (j0 + width) // LIST_ROWS]
+        def entries(list_tile, first, count):
+            return list_tile[:, first // LIST_ROWS : (first + count) // LIST_ROWS]
 
-        def g3(k, t):
+        def y_n3(k, t):
             j0, width = Z_CHUNKS[k]
             return h[t][:, H + j0 : H + j0 + width]
 
-        def fetch1(k, t):
-            nc.scalar.activation(g1[k][:, t, :], y[t][:].indirect(entries(n1_sb, k)), ACT.Copy, scale=0.75)
+        def fetch_n1(k, t):
+            nc.scalar.activation(y_n1[k][:, t, :], y[t][:].indirect(entries(n1_sb, *Z_CHUNKS[k])), ACT.Copy, scale=0.75)
 
-        def fetch3(k, t):
-            nc.scalar.activation(g3(k, t), y[t][:].indirect(entries(n3_sb, k)), ACT.Copy, scale=0.75)
+        def fetch_n3(k, t):
+            nc.scalar.activation(y_n3(k, t), y[t][:].indirect(entries(n3_sb, *Z_CHUNKS[k])), ACT.Copy, scale=0.75)
 
-        def second_term(k, t):
-            nc.vector.tensor_tensor(v_c[k][:, t, :], y[t][:].indirect(entries(n2_sb, k)), g3(k, t), ALU.mult)
+        def make_term_b(k, t):
+            nc.vector.tensor_tensor(term_b[k][:, t, :], y[t][:].indirect(entries(n2_sb, *Z_CHUNKS[k])), y_n3(k, t), ALU.mult)
 
-        def first_term(k, t):
-            j0, width = Z_CHUNKS[k]
-            nc.vector.scalar_tensor_tensor(u_c[k][:, t, :], g1[k][:, t, :], gt_sb[:, t : t + 1], y[t][:, j0 : j0 + width], ALU.mult, ALU.mult)
+        def make_term_a(k, t):
+            nc.vector.scalar_tensor_tensor(
+                term_a[k][:, t, :], y_n1[k][:, t, :], gt_sb[:, t : t + 1], y[t][:, cols_of(Z_CHUNKS[k])], ALU.mult, ALU.mult
+            )
 
-        def summed(k, t):
-            j0, width = Z_CHUNKS[k]
-            nc.vector.scalar_tensor_tensor(z[:, t, j0 : j0 + width], v_c[k][:, t, :], gt_sb[:, t : t + 1], u_c[k][:, t, :], ALU.mult, ALU.add)
+        def make_z(k, t):
+            nc.vector.scalar_tensor_tensor(
+                z[:, t, cols_of(Z_CHUNKS[k])], term_b[k][:, t, :], gt_sb[:, t : t + 1], term_a[k][:, t, :], ALU.mult, ALU.add
+            )
 
-        def woven(k, on_scalar):
-            j0, width = Z_PARTS[k]
-            dst = z_bf[k][:].rearrange("p (c i) t -> p c t i", i=4)
-            src = z[:, :, j0 : j0 + width].rearrange("p t (c i) -> p c t i", i=4)
-            if on_scalar:
-                nc.scalar.copy(dst, src)
-            else:
-                nc.vector.tensor_copy(dst, src)
+        def weave_z(copy, k):
+            weave(copy, z_bf[k], z[:, :, cols_of(PARTS[k])])
 
-        def quantised(k):
-            j0, width = Z_PARTS[k]
-            nc.vector.quantize_mx(out=z_codes[:, j0 : j0 + width].bitcast(FP8X4), scales=z_sc[:, j0 : j0 + width], in_=z_bf[k][:].rearrange("p c t -> p (c t)"))
+        def quantise_z(k):
+            quantise(z_codes[:, cols_of(PARTS[k])], z_sc[:, cols_of(PARTS[k])], z_bf[k])
 
         def second_product(t, cols):
-            nc.tensor.matmul_mx(out=h_bank[t][:, cols], lhsT=w1_deal[:, t, :].bitcast(FP4X4), lhsT_scale=w1s_deal[:, t, :],
-                                rhs=z_codes[:, cols].bitcast(FP8X4), rhs_scale=z_sc[:, cols], start=True, stop=True)
+            nc.tensor.matmul_mx(
+                out=h_bank[t][:, cols], lhsT=w1_deal[:, t, :].bitcast(FP4X4), lhsT_scale=w1s_deal[:, t, :],
+                rhs=z_codes[:, cols].bitcast(FP8X4), rhs_scale=z_sc[:, cols], start=True, stop=True,
+            )
 
-        def bring_h(t, cols, so_far, largest):
-            nc.vector.tensor_scalar(h[t][:, cols], h_bank[t][:, cols], 1.0, so_far, ALU.mult, ALU.max, accum_out=largest)
+        def bring_h(t, cols, top_so_far, top_out):
+            nc.vector.tensor_scalar(h[t][:, cols], h_bank[t][:, cols], 1.0, top_so_far, ALU.mult, ALU.max, accum_out=top_out)
 
         def make_bias(t):
             nc.vector.tensor_scalar(bias[:, t : t + 1], top[t], tau_sb[:, t : t + 1], -1.0, ALU.mult, ALU.mult)
@@ -162,127 +180,126 @@ def tile_picked_tokdotegp_none_po_kernel(tc, x_words, x_scales, wa, gt, w1_words
         out_rows = out_0.rearrange("(p t) j -> p t j", t=PACK)
         out_words = out_1[0].rearrange("p c r -> p (c r)").bitcast(I32)
         o_sc = keep.tile([P, H], U8, name="o_sc", align_bytes=64)
-        n_ch = H // CH
-        ea = [[keep.tile([P, CH, 2, 2], F32, name=f"ea{c}_{t}") for t in range(PACK)] for c in range(n_ch)]
+        ea = [[keep.tile([P, STEP, 2, 2], F32, name=f"ea{c}_{t}") for t in range(PACK)] for c in range(H // STEP)]
         hi = [keep.tile([P, H, 2], F32, name=f"hi{t}") for t in range(PACK)]
         lo = [keep.tile([P, H, 2], F32, name=f"lo{t}") for t in range(PACK)]
         mx = [keep.tile([P, H], F32, name=f"mx{t}") for t in range(PACK)]
         mn = [keep.tile([P, H], F32, name=f"mn{t}") for t in range(PACK)]
-        d = [keep.tile([P, H], F32, name=f"d{t}") for t in range(PACK)]
+        diff = [keep.tile([P, H], F32, name=f"diff{t}") for t in range(PACK)]
         o = keep.tile([P, PACK, H], F32, name="o")
-        o_bf = [keep.tile([P, width, PACK], BF16, name=f"o_bf{j0}", align_bytes=64) for j0, width in O_PARTS]
-        o_codes = [keep.tile([P, width], I32, name=f"o_codes{j0}", align_bytes=64) for j0, width in O_PARTS]
+        o_bf = [keep.tile([P, width, PACK], BF16, name=f"o_bf{j0}", align_bytes=64) for j0, width in PARTS]
+        o_codes = [keep.tile([P, width], I32, name=f"o_codes{j0}", align_bytes=64) for j0, width in PARTS]
 
-        def span(c0, c1):
-            return slice(c0 * CH, c1 * CH)
+        def steps_cols(c0, c1):
+            return slice(c0 * STEP, c1 * STEP)
 
-        def fetch4(c, t):
-            nc.scalar.activation(ea[c][t][:].rearrange("p j a b -> p (j a b)"), h[t][:].indirect(n4_sb[:, c * 32 : (c + 1) * 32]), ACT.Exp,
-                                 bias=bias[:, t : t + 1], scale=tau_sb[:, t : t + 1])
+        def fetch_ea(c, t):
+            nc.scalar.activation(
+                ea[c][t][:].rearrange("p j a b -> p (j a b)"),
+                h[t][:].indirect(entries(n4_sb, c * STEP * MEMBERS, STEP * MEMBERS)),
+                ACT.Exp, bias=bias[:, t : t + 1], scale=tau_sb[:, t : t + 1],
+            )
 
-        def pair_hi(c, t):
-            nc.vector.tensor_tensor(hi[t][:, span(c, c + 1), :], ea[c][t][:, :, 0, :], ea[c][t][:, :, 1, :], ALU.max)
+        def make_hi(c, t):
+            nc.vector.tensor_tensor(hi[t][:, steps_cols(c, c + 1), :], ea[c][t][:, :, 0, :], ea[c][t][:, :, 1, :], ALU.max)
 
-        def pair_lo(c, t):
-            nc.vector.tensor_tensor(lo[t][:, span(c, c + 1), :], ea[c][t][:, :, 0, :], ea[c][t][:, :, 1, :], ALU.min)
+        def make_lo(c, t):
+            nc.vector.tensor_tensor(lo[t][:, steps_cols(c, c + 1), :], ea[c][t][:, :, 0, :], ea[c][t][:, :, 1, :], ALU.min)
 
-        def largest(t, cols):
+        def make_mx(t, cols):
             nc.vector.tensor_tensor(mx[t][:, cols], hi[t][:, cols, 0], hi[t][:, cols, 1], ALU.max)
 
-        def smallest(t, cols):
+        def make_mn(t, cols):
             nc.vector.tensor_tensor(mn[t][:, cols], lo[t][:, cols, 0], lo[t][:, cols, 1], ALU.min)
 
-        def spread(t, cols):
-            nc.vector.tensor_tensor(d[t][:, cols], mx[t][:, cols], mn[t][:, cols], ALU.subtract)
+        def make_diff(t, cols):
+            nc.vector.tensor_tensor(diff[t][:, cols], mx[t][:, cols], mn[t][:, cols], ALU.subtract)
 
-        def result(t, cols):
-            nc.vector.scalar_tensor_tensor(o[:, t, cols], d[t][:, cols], 3.0, h_bank[t][:, cols], ALU.mult, ALU.mult)
+        def make_out(t, cols):
+            nc.vector.scalar_tensor_tensor(o[:, t, cols], diff[t][:, cols], 3.0, h_bank[t][:, cols], ALU.mult, ALU.mult)
 
-        def store(ts, cols):
-            nc.sync.dma_start(out_rows[:, ts, cols], o[:, ts, cols])
+        def store_out(t, cols):
+            nc.sync.dma_start(out_rows[:, t : t + 1, cols], o[:, t : t + 1, cols])
 
-        def rounded(k, on_scalar):
-            j0, width = O_PARTS[k]
-            dst = o_bf[k][:].rearrange("p (c i) t -> p c t i", i=4)
-            src = o[:, :, j0 : j0 + width].rearrange("p t (c i) -> p c t i", i=4)
-            if on_scalar:
-                nc.scalar.copy(dst, src)
-            else:
-                nc.vector.tensor_copy(dst, src)
+        def weave_out(copy, k):
+            weave(copy, o_bf[k], o[:, :, cols_of(PARTS[k])])
 
-        def planes(k):
-            j0, width = O_PARTS[k]
-            nc.vector.quantize_mx(out=o_codes[k][:].bitcast(FP8X4), scales=o_sc[:, j0 : j0 + width], in_=o_bf[k][:].rearrange("p c t -> p (c t)"))
-            nc.sync.dma_start(out_words[:, j0 : j0 + width], o_codes[k][:])
+        def planes_of_out(k):
+            quantise(o_codes[k][:], o_sc[:, cols_of(PARTS[k])], o_bf[k])
+            nc.sync.dma_start(out_words[:, cols_of(PARTS[k])], o_codes[k][:])
 
         nc.scalar.copy(y[0][:], y_bank[0][:])
         for t in range(1, PACK):
             nc.vector.tensor_copy(y[t][:], y_bank[t][:])
-        steps = [(k, t) for k in range(len(Z_CHUNKS)) for t in range(PACK)]
-        for n, (k, t) in enumerate(steps):
-            fetch3(k, t)
-            fetch1(k, t)
-            second_term(k, t)
+
+        turns = [(k, t) for k in range(len(Z_CHUNKS)) for t in range(PACK)]
+        for n, (k, t) in enumerate(turns):
+            fetch_n3(k, t)
+            fetch_n1(k, t)
+            make_term_b(k, t)
             if n > 0:
-                summed(*steps[n - 1])
-            first_term(k, t)
-        woven(0, True)
-        woven(1, True)
-        quantised(0)
-        summed(*steps[-1])
-        second_product(0, slice(0, 256))
-        woven(2, False)
-        quantised(1)
-        quantised(2)
-        bring_h(0, slice(0, 256), None, early[:])
-        second_product(0, slice(256, H))
-        bring_h(0, slice(256, H), early[:], top[0])
+                make_z(*turns[n - 1])
+            make_term_a(k, t)
+
+        weave_z(nc.scalar.copy, 0)
+        weave_z(nc.scalar.copy, 1)
+        quantise_z(0)
+        make_z(*turns[-1])
+        second_product(0, first_half)
+        weave_z(nc.vector.tensor_copy, 2)
+        quantise_z(1)
+        quantise_z(2)
+        bring_h(0, first_half, None, top_first_half[:])
+        second_product(0, second_half)
+        bring_h(0, second_half, top_first_half[:], top[0])
         make_bias(0)
         for t in range(1, PACK):
-            second_product(t, slice(0, H))
-            bring_h(t, slice(0, H), None, top[t])
+            second_product(t, whole_row)
+            bring_h(t, whole_row, None, top[t])
             make_bias(t)
-        units = [(c0, t) for t in range(PACK) for c0 in (0, 2)]
-        for c0, t in units:
-            fetch4(c0, t)
-            fetch4(c0 + 1, t)
+
+        halves = [(c0, t) for t in range(PACK) for c0 in (0, 2)]
+        for c0, t in halves:
+            fetch_ea(c0, t)
+            fetch_ea(c0 + 1, t)
         before = None
-        for c0, t in units[:-1]:
-            pair_hi(c0, t)
+        for c0, t in halves[:-1]:
+            make_hi(c0, t)
             if before:
-                spread(*before)
-            pair_lo(c0, t)
+                make_diff(*before)
+            make_lo(c0, t)
             if before:
-                result(*before)
-                store(slice(before[0], before[0] + 1), before[1])
-            pair_hi(c0 + 1, t)
-            pair_lo(c0 + 1, t)
-            before = (t, span(c0, c0 + 2))
-            largest(*before)
-            smallest(*before)
-        last = PACK - 1
-        pair_hi(2, last)
-        spread(*before)
-        pair_lo(2, last)
-        result(*before)
-        store(slice(before[0], before[0] + 1), before[1])
-        rounded(0, True)
-        pair_hi(3, last)
-        largest(last, span(2, 3))
-        smallest(last, span(2, 3))
-        pair_lo(3, last)
-        spread(last, span(2, 3))
-        largest(last, span(3, 4))
-        result(last, span(2, 3))
-        rounded(1, True)
-        smallest(last, span(3, 4))
-        planes(0)
-        spread(last, span(3, 4))
-        result(last, span(3, 4))
-        store(slice(last, last + 1), span(2, 4))
-        planes(1)
-        rounded(2, False)
-        planes(2)
-        for q in range(4):
-            eng = nc.scalar if q % 2 else nc.sync
-            eng.dma_start(out_2[0, 4 * q : 4 * q + 4, :].bitcast(I32), o_sc[32 * q : 32 * q + 4, :].bitcast(I32))
+                make_out(*before)
+                store_out(*before)
+            make_hi(c0 + 1, t)
+            make_lo(c0 + 1, t)
+            before = (t, steps_cols(c0, c0 + 2))
+            make_mx(*before)
+            make_mn(*before)
+
+        step_2, step_3 = steps_cols(2, 3), steps_cols(3, 4)
+        make_hi(2, LAST)
+        make_diff(*before)
+        make_lo(2, LAST)
+        make_out(*before)
+        store_out(*before)
+        weave_out(nc.scalar.copy, 0)
+        make_hi(3, LAST)
+        make_mx(LAST, step_2)
+        make_mn(LAST, step_2)
+        make_lo(3, LAST)
+        make_diff(LAST, step_2)
+        make_mx(LAST, step_3)
+        make_out(LAST, step_2)
+        weave_out(nc.scalar.copy, 1)
+        make_mn(LAST, step_3)
+        planes_of_out(0)
+        make_diff(LAST, step_3)
+        make_out(LAST, step_3)
+        store_out(LAST, second_half)
+        planes_of_out(1)
+        weave_out(nc.vector.tensor_copy, 2)
+        planes_of_out(2)
+        for q in range(QUADS):
+            queue = nc.scalar if q % 2 else nc.sync
+            queue.dma_start(out_2[0, 4 * q : 4 * q + 4, :].bitcast(I32), o_sc[32 * q : 32 * q + 4, :].bitcast(I32))

from contextlib import ExitStack

import concourse.mybir as mybir

K, T, S, N, H, W = 512, 2048, 512, 512, 512, 2048
FLOPS = 2 * K * S * H + 2 * S * N * H

F32 = mybir.dt.float32
BF16 = mybir.dt.bfloat16
I32 = mybir.dt.int32
U32 = mybir.dt.uint32
U16 = mybir.dt.uint16
U8 = mybir.dt.uint8
FP8X4 = mybir.dt.float8_e4m3fn_x4
FP4X4 = mybir.dt.float4_e2m1fn_x4
ALU = mybir.AluOpType
ACT = mybir.ActivationFunctionType

P = 128
PACK = 4
QUADS = 4
LIST_ROWS = 16
MEMBERS = W // H
RUN = 4
HALF = H // 2
STEP = 128
LAST = PACK - 1

WA_LOADS = [(0, HALF), (HALF, HALF)]
PARTS = [(0, HALF), (HALF, STEP), (HALF + STEP, STEP)]
Z_CHUNKS = [(0, H - STEP), (H - STEP, STEP)]


def tile_picked_tokdotegp_none_po_kernel(
    tc, x_words, x_scales, wa, gt, w1_words, w1_scales, tau, offs, n1, n2, n3, n4, out_0, out_1, out_2
):
    nc = tc.nc
    with ExitStack() as ctx:
        keep = ctx.enter_context(tc.tile_pool(name="keep", bufs=1))
        psum = ctx.enter_context(tc.psum_pool(name="psum", bufs=1))

        def weave(copy, woven_tile, row_sets):
            copy(woven_tile[:].rearrange("p (c i) t -> p c t i", i=RUN), row_sets.rearrange("p t (c i) -> p c t i", i=RUN))

        def scalar_cast(out, in_):
            nc.scalar.activation(out, in_, ACT.Copy)

        def quantise(codes, scales, woven_tile):
            nc.vector.quantize_mx(out=codes.bitcast(FP8X4), scales=scales, in_=woven_tile[:].rearrange("p j t -> p (j t)"))

        def cols_of(part):
            return slice(part[0], part[0] + part[1])

        offs_sb = keep.tile([P, S // LIST_ROWS], U16, name="offs_sb")
        n1_sb = keep.tile([P, H // LIST_ROWS], U16, name="n1_sb")
        n2_sb = keep.tile([P, H // LIST_ROWS], U16, name="n2_sb")
        n3_sb = keep.tile([P, H // LIST_ROWS], U16, name="n3_sb")
        n4_sb = keep.tile([P, W // LIST_ROWS], U16, name="n4_sb")
        x_all = keep.tile([P, T], I32, name="x_all")
        xs_all = keep.tile([P, T], U8, name="xs_all")
        wa_raw = [keep.tile([P, PACK, width], F32, name=f"wa_raw{j0}") for j0, width in WA_LOADS]
        w1_raw = keep.tile([P, 2 * N], U8, name="w1_raw")
        w1s_raw = keep.tile([P, N], U8, name="w1s_raw")
        gt_sb = keep.tile([P, PACK], F32, name="gt_sb")
        tau_sb = keep.tile([P, PACK], F32, name="tau_sb")

        def load_scale_rows(tile, scales):
            for q in range(QUADS):
                nc.sync.dma_start(tile[32 * q : 32 * q + 4, :].bitcast(I32), scales[0, 4 * q : 4 * q + 4, :].bitcast(I32))

        nc.vector.memset(xs_all[:].bitcast(I32), 0)
        nc.gpsimd.memset(w1s_raw[:].bitcast(I32), 0)
        nc.sync.dma_start(offs_sb[:], offs)
        load_scale_rows(xs_all, x_scales)
        wa_rows = wa.rearrange("(p r) h -> p r h", r=PACK)
        nc.sync.dma_start(wa_raw[0][:], wa_rows[:, :, cols_of(WA_LOADS[0])])
        nc.sync.dma_start(n3_sb[:], n3)
        nc.sync.dma_start(x_all[:], x_words[0].rearrange("p c r -> p (c r)").bitcast(I32))
        nc.sync.dma_start(wa_raw[1][:], wa_rows[:, :, cols_of(WA_LOADS[1])])
        nc.sync.dma_start(w1_raw[:].bitcast(I32), w1_words[0].bitcast(I32))
        nc.sync.dma_start(n1_sb[:], n1)
        nc.sync.dma_start(n2_sb[:], n2)
        nc.sync.dma_start(gt_sb[:], gt.rearrange("(p t) o -> p (t o)", t=PACK))
        load_scale_rows(w1s_raw, w1_scales)
        nc.sync.dma_start(tau_sb[:], tau.rearrange("(p t) o -> p (t o)", t=PACK))
        nc.sync.dma_start(n4_sb[:], n4)

        xs_pick = keep.tile([P, PACK, P], U8, name="xs_pick", align_bytes=64)
        x_pick = keep.tile([P, PACK, P], U32, name="x_pick", align_bytes=64)
        nc.vector.tensor_copy(xs_pick[:].rearrange("p t m -> p m t"), xs_all[:].indirect(offs_sb[:]))
        nc.vector.tensor_copy(x_pick[:].rearrange("p t m -> p m t"), x_all[:].bitcast(U32).indirect(offs_sb[:]))

        w1_deal = keep.tile([P, PACK, 2 * P], U8, name="w1_deal", align_bytes=64)
        w1s_deal = keep.tile([P, PACK, P], U8, name="w1s_deal", align_bytes=64)

        wa_bf = [keep.tile([P, width, PACK], BF16, name=f"wa_bf{j0}", align_bytes=64) for j0, width in PARTS]
        wa_codes = keep.tile([P, H], U32, name="wa_codes", align_bytes=64)
        wa_sc = keep.tile([P, H], U8, name="wa_sc", align_bytes=64)
        weave(scalar_cast, wa_bf[0], wa_raw[0][:])
        weave(scalar_cast, wa_bf[1], wa_raw[1][:, :, :STEP])
        weave(nc.vector.tensor_copy, wa_bf[2], wa_raw[1][:, :, STEP:])
        for k in (0, 2, 1):
            quantise(wa_codes[:, cols_of(PARTS[k])], wa_sc[:, cols_of(PARTS[k])], wa_bf[k])

        nc.scalar.copy(
            w1_deal[:].rearrange("p t b -> p (t b)").bitcast(U16).rearrange("p (t m) -> p t m", t=PACK),
            w1_raw[:].bitcast(U16).rearrange("p (m t) -> p t m", t=PACK),
        )
        nc.vector.tensor_copy(w1s_deal[:].rearrange("p t m -> p m t"), w1s_raw[:].rearrange("p (m t) -> p m t", t=PACK))

        whole_row = slice(0, H)
        first_half, second_half = slice(0, HALF), slice(HALF, H)
        y_bank = [psum.tile([P, H], F32, name=f"y_bank{t}") for t in range(PACK)]
        for t in range(PACK):
            for cols in [first_half, second_half] if t == 0 else [whole_row]:
                nc.tensor.matmul_mx(
                    out=y_bank[t][:, cols], lhsT=x_pick[:, t, :].bitcast(FP8X4), lhsT_scale=xs_pick[:, t, :],
                    rhs=wa_codes[:, cols].bitcast(FP8X4), rhs_scale=wa_sc[:, cols], start=True, stop=True,
                )

        y = [keep.tile([P, H], F32, name=f"y{t}") for t in range(PACK)]
        h = [keep.tile([P, 2 * H], F32, name=f"h{t}") for t in range(PACK)]
        h_bank = [psum.tile([P, H], F32, name=f"h_bank{t}") for t in range(PACK)]
        top_first_half = keep.tile([P, 1], F32, name="top_first_half")
        tops = keep.tile([P, LAST], F32, name="tops")
        top = [tops[:, max(t - 1, 0) : max(t - 1, 0) + 1] for t in range(PACK)]
        bias = keep.tile([P, PACK], F32, name="bias")
        y_n1 = [keep.tile([P, PACK, width], F32, name=f"y_n1_{j0}") for j0, width in Z_CHUNKS]
        term_a = [keep.tile([P, PACK, width], F32, name=f"term_a{j0}") for j0, width in Z_CHUNKS]
        term_b = [keep.tile([P, PACK, width], F32, name=f"term_b{j0}") for j0, width in Z_CHUNKS]
        z = keep.tile([P, PACK, H], BF16, name="z")
        z_bf = [keep.tile([P, width, PACK], BF16, name=f"z_bf{j0}", align_bytes=64) for j0, width in PARTS]
        z_codes = keep.tile([P, H], U32, name="z_codes", align_bytes=64)
        z_sc = keep.tile([P, H], U8, name="z_sc", align_bytes=64)

        def entries(list_tile, first, count):
            return list_tile[:, first // LIST_ROWS : (first + count) // LIST_ROWS]

        def y_n3(k, t):
            j0, width = Z_CHUNKS[k]
            return h[t][:, H + j0 : H + j0 + width]

        def fetch_n1(k, t):
            nc.scalar.activation(y_n1[k][:, t, :], y[t][:].indirect(entries(n1_sb, *Z_CHUNKS[k])), ACT.Copy, scale=0.75)

        def fetch_n3(k, t):
            nc.scalar.activation(y_n3(k, t), y[t][:].indirect(entries(n3_sb, *Z_CHUNKS[k])), ACT.Copy, scale=0.75)

        def make_term_b(k, t):
            nc.vector.tensor_tensor(term_b[k][:, t, :], y[t][:].indirect(entries(n2_sb, *Z_CHUNKS[k])), y_n3(k, t), ALU.mult)

        def make_term_a(k, t):
            nc.vector.scalar_tensor_tensor(
                term_a[k][:, t, :], y_n1[k][:, t, :], gt_sb[:, t : t + 1], y[t][:, cols_of(Z_CHUNKS[k])], ALU.mult, ALU.mult
            )

        def make_z(k, t):
            nc.vector.scalar_tensor_tensor(
                z[:, t, cols_of(Z_CHUNKS[k])], term_b[k][:, t, :], gt_sb[:, t : t + 1], term_a[k][:, t, :], ALU.mult, ALU.add
            )

        def weave_z(copy, k):
            weave(copy, z_bf[k], z[:, :, cols_of(PARTS[k])])

        def quantise_z(k):
            quantise(z_codes[:, cols_of(PARTS[k])], z_sc[:, cols_of(PARTS[k])], z_bf[k])

        def second_product(t, cols):
            nc.tensor.matmul_mx(
                out=h_bank[t][:, cols], lhsT=w1_deal[:, t, :].bitcast(FP4X4), lhsT_scale=w1s_deal[:, t, :],
                rhs=z_codes[:, cols].bitcast(FP8X4), rhs_scale=z_sc[:, cols], start=True, stop=True,
            )

        def bring_h(t, cols, top_so_far, top_out):
            nc.vector.tensor_scalar(h[t][:, cols], h_bank[t][:, cols], 1.0, top_so_far, ALU.mult, ALU.max, accum_out=top_out)

        def make_bias(t):
            nc.vector.tensor_scalar(bias[:, t : t + 1], top[t], tau_sb[:, t : t + 1], -1.0, ALU.mult, ALU.mult)

        out_rows = out_0.rearrange("(p t) j -> p t j", t=PACK)
        out_words = out_1[0].rearrange("p c r -> p (c r)").bitcast(I32)
        o_sc = keep.tile([P, H], U8, name="o_sc", align_bytes=64)
        ea = [[keep.tile([P, STEP, 2, 2], F32, name=f"ea{c}_{t}") for t in range(PACK)] for c in range(H // STEP)]
        hi = [keep.tile([P, H, 2], F32, name=f"hi{t}") for t in range(PACK)]
        lo = [keep.tile([P, H, 2], F32, name=f"lo{t}") for t in range(PACK)]
        mx = [keep.tile([P, H], F32, name=f"mx{t}") for t in range(PACK)]
        mn = [keep.tile([P, H], F32, name=f"mn{t}") for t in range(PACK)]
        diff = [keep.tile([P, H], F32, name=f"diff{t}") for t in range(PACK)]
        o = keep.tile([P, PACK, H], F32, name="o")
        o_bf = [keep.tile([P, width, PACK], BF16, name=f"o_bf{j0}", align_bytes=64) for j0, width in PARTS]
        o_codes = [keep.tile([P, width], I32, name=f"o_codes{j0}", align_bytes=64) for j0, width in PARTS]

        def steps_cols(c0, c1):
            return slice(c0 * STEP, c1 * STEP)

        def fetch_ea(c, t):
            nc.scalar.activation(
                ea[c][t][:].rearrange("p j a b -> p (j a b)"),
                h[t][:].indirect(entries(n4_sb, c * STEP * MEMBERS, STEP * MEMBERS)),
                ACT.Exp, bias=bias[:, t : t + 1], scale=tau_sb[:, t : t + 1],
            )

        def make_hi(c, t):
            nc.vector.tensor_tensor(hi[t][:, steps_cols(c, c + 1), :], ea[c][t][:, :, 0, :], ea[c][t][:, :, 1, :], ALU.max)

        def make_lo(c, t):
            nc.vector.tensor_tensor(lo[t][:, steps_cols(c, c + 1), :], ea[c][t][:, :, 0, :], ea[c][t][:, :, 1, :], ALU.min)

        def make_mx(t, cols):
            nc.vector.tensor_tensor(mx[t][:, cols], hi[t][:, cols, 0], hi[t][:, cols, 1], ALU.max)

        def make_mn(t, cols):
            nc.vector.tensor_tensor(mn[t][:, cols], lo[t][:, cols, 0], lo[t][:, cols, 1], ALU.min)

        def make_diff(t, cols):
            nc.vector.tensor_tensor(diff[t][:, cols], mx[t][:, cols], mn[t][:, cols], ALU.subtract)

        def make_out(t, cols):
            nc.vector.scalar_tensor_tensor(o[:, t, cols], diff[t][:, cols], 3.0, h_bank[t][:, cols], ALU.mult, ALU.mult)

        def store_out(t, cols):
            nc.sync.dma_start(out_rows[:, t : t + 1, cols], o[:, t : t + 1, cols])

        def weave_out(copy, k):
            weave(copy, o_bf[k], o[:, :, cols_of(PARTS[k])])

        def planes_of_out(k):
            quantise(o_codes[k][:], o_sc[:, cols_of(PARTS[k])], o_bf[k])
            nc.sync.dma_start(out_words[:, cols_of(PARTS[k])], o_codes[k][:])

        nc.scalar.copy(y[0][:], y_bank[0][:])
        for t in range(1, PACK):
            nc.vector.tensor_copy(y[t][:], y_bank[t][:])

        turns = [(k, t) for k in range(len(Z_CHUNKS)) for t in range(PACK)]
        for n, (k, t) in enumerate(turns):
            fetch_n3(k, t)
            fetch_n1(k, t)
            make_term_b(k, t)
            if n > 0:
                make_z(*turns[n - 1])
            make_term_a(k, t)

        weave_z(nc.scalar.copy, 0)
        weave_z(nc.scalar.copy, 1)
        quantise_z(0)
        make_z(*turns[-1])
        second_product(0, first_half)
        weave_z(nc.vector.tensor_copy, 2)
        quantise_z(1)
        quantise_z(2)
        bring_h(0, first_half, None, top_first_half[:])
        second_product(0, second_half)
        bring_h(0, second_half, top_first_half[:], top[0])
        make_bias(0)
        for t in range(1, PACK):
            second_product(t, whole_row)
            bring_h(t, whole_row, None, top[t])
            make_bias(t)

        halves = [(c0, t) for t in range(PACK) for c0 in (0, 2)]
        for c0, t in halves:
            fetch_ea(c0, t)
            fetch_ea(c0 + 1, t)
        before = None
        for c0, t in halves[:-1]:
            make_hi(c0, t)
            if before:
                make_diff(*before)
            make_lo(c0, t)
            if before:
                make_out(*before)
                store_out(*before)
            make_hi(c0 + 1, t)
            make_lo(c0 + 1, t)
            before = (t, steps_cols(c0, c0 + 2))
            make_mx(*before)
            make_mn(*before)

        step_2, step_3 = steps_cols(2, 3), steps_cols(3, 4)
        make_hi(2, LAST)
        make_diff(*before)
        make_lo(2, LAST)
        make_out(*before)
        store_out(*before)
        weave_out(nc.scalar.copy, 0)
        make_hi(3, LAST)
        make_mx(LAST, step_2)
        make_mn(LAST, step_2)
        make_lo(3, LAST)
        make_diff(LAST, step_2)
        make_mx(LAST, step_3)
        make_out(LAST, step_2)
        weave_out(nc.scalar.copy, 1)
        make_mn(LAST, step_3)
        planes_of_out(0)
        make_diff(LAST, step_3)
        make_out(LAST, step_3)
        store_out(LAST, second_half)
        planes_of_out(1)
        weave_out(nc.vector.tensor_copy, 2)
        planes_of_out(2)
        for q in range(QUADS):
            queue = nc.scalar if q % 2 else nc.sync
            queue.dma_start(out_2[0, 4 * q : 4 * q + 4, :].bitcast(I32), o_sc[32 * q : 32 * q + 4, :].bitcast(I32))
